import numpy as np
import ml_dtypes


def mxq(x, axis, fmt="e4m3"):
    dtype, down = {"e4m3": (ml_dtypes.float8_e4m3fn, 7), "e5m2": (ml_dtypes.float8_e5m2, 14)}[fmt]
    v = np.moveaxis(np.asarray(x, np.float32).astype(ml_dtypes.bfloat16).astype(np.float64), axis, -1)
    blocks = v.reshape(v.shape[:-1] + (-1, 32))
    amax = np.abs(blocks).max(-1, keepdims=True)
    byte = np.maximum(np.where(amax > 0, np.frexp(amax)[1] - 1 + 127, 0) - down, 1)
    scale = np.exp2(byte - 127.0)
    codes = (blocks / scale).astype(np.float32).astype(dtype).astype(np.float64)
    return np.moveaxis((codes * scale).reshape(v.shape), -1, axis)


WIDE = False


def mx_kscale(k):
    if not WIDE:
        return np.ones(k)
    levels = np.array([10, -10, 5, -5, 0])
    if k % 512:
        return np.exp2(np.random.permutation(np.resize(levels, k // 32))).repeat(32)
    a = np.empty((k // 512, 16))
    for p in range(k // 512):
        a[p, :8] = np.random.permutation(np.resize(levels, 8))
        for g in range(8):
            far = levels[np.abs(levels - a[p, g]) >= 10]
            a[p, g + 8] = far[np.random.randint(len(far))]
    return np.exp2(a.ravel()).repeat(32)


def f64(x):
    return np.asarray(x).astype(np.float64)


def striped(idx):
    return np.tile(idx.reshape(-1, 16).T, (8, 1)).astype(np.uint16)


def unstriped(offs):
    return offs[:16].T.reshape(-1).astype(np.int64)


E2M1 = np.array([0.0, 0.5, 1.0, 1.5, 2.0, 3.0, 4.0, 6.0, -0.0, -0.5, -1.0, -1.5, -2.0, -3.0, -4.0, -6.0])


def pack_weight(w, fmt):
    k, n = w.shape
    w = f64(np.asarray(w, np.float32).astype(ml_dtypes.bfloat16)).reshape(k // 32, 32, n)
    amax = np.abs(w).max(1)
    if fmt == "e4m3":
        byte = np.frexp(amax)[1] - 1 + 127 - 7
    else:
        mant, ex = np.frexp(amax / 6.0)
        byte = np.where(mant > 0.5, ex, ex - 1) + 127
    byte = np.clip(np.where(amax > 0, byte, 1), 1, 254)
    scaled = (w * np.exp2(127.0 - byte)[:, None, :]).reshape(k, n).astype(np.float32)
    by_word = np.ascontiguousarray(scaled.reshape(k // 512, 128, 4, n).transpose(0, 1, 3, 2))
    if fmt == "e4m3":
        words = by_word.astype(ml_dtypes.float8_e4m3fn).view(np.uint8)
    else:
        c = by_word.astype(ml_dtypes.float4_e2m1fn).view(np.uint8) & 0xF
        words = (c[..., 0::2] | (c[..., 1::2] << 4)).reshape(k // 512, 128, 2 * n)
    return np.ascontiguousarray(words), np.ascontiguousarray(byte.astype(np.uint8).reshape(k // 512, 16, n))


def unpack_weight(words, scales, fmt):
    g, _, n = scales.shape
    words = np.ascontiguousarray(words).reshape(g, 128, n, -1)
    if fmt == "e4m3":
        vals = words.view(ml_dtypes.float8_e4m3fn).astype(np.float64)
    else:
        nib = np.empty((g, 128, n, 4), np.uint8)
        nib[..., 0::2] = words & 0xF
        nib[..., 1::2] = words >> 4
        vals = E2M1[nib]
    vals = vals * np.repeat(np.exp2(scales.astype(np.float64) - 127.0), 8, axis=1)[..., None]
    return vals.transpose(0, 1, 3, 2).reshape(g * 512, n)


def gelu(v):
    return 0.5 * v * (1.0 + np.tanh(np.sqrt(2.0 / np.pi) * (v + 0.044715 * v**3)))


def bf(x):
    return np.asarray(x, np.float32).astype(ml_dtypes.bfloat16)


def planes(Y):
    n, m = Y.shape
    b = f64(bf(Y)).reshape(n // 32, 32, m)
    amax = np.abs(b).max(1)
    byte = np.clip(np.where(amax > 0, np.frexp(amax)[1] - 1 + 127 - 7, 1), 1, 254)
    codes = (b * np.exp2(127.0 - byte)[:, None, :]).reshape(n, m).astype(np.float32).astype(ml_dtypes.float8_e4m3fn).view(np.uint8)
    words = codes.reshape(n // 512, 128, 4, m).transpose(0, 1, 3, 2)
    return np.ascontiguousarray(words), np.ascontiguousarray(byte.astype(np.uint8).reshape(n // 512, 16, m))


K, T, S, H, N, P = 1024, 4096, 1024, 512, 1024, 512

def setup_inputs():
    n = np.random.standard_normal
    s = mx_kscale(K)[:, None]
    u = mx_kscale(H)[:, None]
    d = {}
    d["tab_words"], d["tab_scales"] = pack_weight(n((K, T)) * s, "e4m3")
    d["offs"] = striped(np.random.permutation(T)[:S])
    d["pos1"] = striped(np.random.permutation(S)[:P])
    d["pos2"] = striped(np.random.permutation(S)[:P])
    d["w1"] = (n((K, H)) / s / K ** 0.5).astype(np.float32)
    d["w2_words"], d["w2_scales"] = pack_weight(n((K, H)) / s / K ** 0.5, "e4m3")
    d["w3"] = (n((K, H)) / s / K ** 0.5).astype(np.float32)
    d["gh"] = (np.exp(0.5 * n(H)) * u[:, 0]).astype(np.float32)
    d["w4_words"], d["w4_scales"] = pack_weight(n((H, N)) / u / H ** 0.5, "e2m1")
    d["wear"] = n((N, S)).astype(np.float32)
    d["gy"] = np.exp(0.8 * n(N)).astype(np.float32)
    return d

def reference(tab_words, tab_scales, offs, pos1, pos2, w1, w2_words, w2_scales, w3, gh, w4_words, w4_scales, wear, gy):
    v = unpack_weight(tab_words, tab_scales, "e4m3")[:, unstriped(offs)]
    w2 = unpack_weight(w2_words, w2_scales, "e4m3")
    w4 = unpack_weight(w4_words, w4_scales, "e2m1")
    a = mxq(f64(w1), 0, "e4m3").T @ v
    b = w2.T @ v
    e = mxq(f64(w3), 0, "e4m3").T @ v
    h = np.maximum(np.minimum(a, b), e) * f64(gh)[:, None]
    g2 = (w4.T @ mxq(h, 0, "e4m3")) * f64(wear)
    y = np.tanh(g2[:, unstriped(pos1)] + g2[:, unstriped(pos2)]) * f64(gy)[:, None]
    words, scales = planes(y)
    return y, words, scales

@@ -1,0 +1,260 @@
+from contextlib import ExitStack
+
+import concourse.mybir as mybir
+
+K, T, S, H, N, M = 1024, 4096, 1024, 512, 1024, 512
+FLOPS = 2 * (3 * K * H * S + H * N * S)
+
+F32 = mybir.dt.float32
+BF16 = mybir.dt.bfloat16
+I32 = mybir.dt.int32
+U32 = mybir.dt.uint32
+U16 = mybir.dt.uint16
+U8 = mybir.dt.uint8
+FP8X4 = mybir.dt.float8_e4m3fn_x4
+FP4X4 = mybir.dt.float4_e2m1fn_x4
+ALU = mybir.AluOpType
+ACT = mybir.ActivationFunctionType
+
+P = 128
+PACK = 4
+PASS = P * PACK
+BANK = 512
+LIST_ROWS = 16
+QUADS = 4
+
+
+def tile_list_zipper_tooth_features_kernel(
+    tc, tab_words, tab_scales, offs, pos1, pos2, w1, w2_words, w2_scales, w3, gh,
+    w4_words, w4_scales, wear, gy, out_0, out_1, out_2,
+):
+    nc = tc.nc
+    passes = K // PASS
+    halves = S // BANK
+    groups = N // PASS
+
+    with ExitStack() as ctx:
+        keep = ctx.enter_context(tc.tile_pool(name="keep", bufs=1))
+        wide = ctx.enter_context(tc.tile_pool(name="wide", bufs=4))
+        ring = ctx.enter_context(tc.tile_pool(name="ring", bufs=3))
+        psum = ctx.enter_context(tc.psum_pool(name="psum", bufs=4))
+
+        tab_plane = keep.tile([P, T], U8, name="tab_plane", align_bytes=64)
+        w2_plane_raw = keep.tile([P, H], U8, name="w2_plane_raw", align_bytes=64)
+        w4_plane_raw = keep.tile([P, N], U8, name="w4_plane_raw", align_bytes=64)
+        for plane in (w2_plane_raw, tab_plane, w4_plane_raw):
+            nc.vector.memset(plane[:].bitcast(I32), 0)
+
+        w2_raw = keep.tile([P, passes, H], I32, name="w2_raw")
+        nc.sync.dma_start(out=w2_raw[:], in_=w2_words.rearrange("a p c i -> p a (c i)").bitcast(I32))
+        w4_raw = keep.tile([P, 2 * N], U8, name="w4_raw")
+        nc.sync.dma_start(out=w4_raw[:].bitcast(I32), in_=w4_words[0].bitcast(I32))
+        idx = keep.tile([P, S // LIST_ROWS], U16, name="idx")
+        nc.sync.dma_start(idx[:], offs)
+        left = keep.tile([P, M // LIST_ROWS], U16, name="left")
+        nc.sync.dma_start(left[:], pos1)
+        right = keep.tile([P, M // LIST_ROWS], U16, name="right")
+        nc.sync.dma_start(right[:], pos2)
+        gh_sb = keep.tile([P, PACK], F32, name="gh_sb")
+        nc.sync.dma_start(out=gh_sb[:], in_=gh.rearrange("(p t) -> p t", t=PACK))
+        gy_sb = keep.tile([P, groups, PACK], F32, name="gy_sb")
+        nc.sync.dma_start(out=gy_sb[:], in_=gy.rearrange("(g p t) -> p g t", g=groups, t=PACK))
+
+        tab = [keep.tile([P, T], I32, name="tab%d" % a, tag="tab%d" % a, align_bytes=64) for a in range(passes)]
+        nc.sync.dma_start(out=tab[0][:], in_=tab_words[0].rearrange("p t i -> p (t i)").bitcast(I32))
+        for q in range(QUADS):
+            nc.scalar.dma_start(
+                out=w2_plane_raw[32 * q : 32 * q + 4 * passes, :].bitcast(I32),
+                in_=w2_scales[:, 4 * q : 4 * q + 4, :].bitcast(I32),
+            )
+        for q in range(QUADS):
+            nc.scalar.dma_start(
+                out=tab_plane[32 * q : 32 * q + 4 * passes, :].bitcast(I32),
+                in_=tab_scales[:, 4 * q : 4 * q + 4, :].bitcast(I32),
+            )
+        nc.sync.dma_start(out=tab[1][:], in_=tab_words[1].rearrange("p t i -> p (t i)").bitcast(I32))
+
+        raw = {}
+        for name, w in (("w1", w1), ("w3", w3)):
+            for a in range(passes):
+                raw[name, a] = wide.tile([P, PACK, H], F32, name="raw", tag="f32x4")
+                nc.sync.dma_start(
+                    out=raw[name, a][:], in_=w[a * PASS : (a + 1) * PASS, :].rearrange("(p i) c -> p i c", i=PACK)
+                )
+        for q in range(QUADS):
+            nc.sync.dma_start(
+                out=w4_plane_raw[32 * q : 32 * q + 4, :].bitcast(I32),
+                in_=w4_scales[0, 4 * q : 4 * q + 4, :].bitcast(I32),
+            )
+        wear_rows = wear.rearrange("(g p t) j -> g p t j", g=groups, t=PACK)
+        wear_sb = {}
+        for g in range(groups):
+            for u in range(2):
+                pair = keep.tile([P, 2, S], F32, name="wear%d%d" % (g, u))
+                nc.sync.dma_start(out=pair[:], in_=wear_rows[g, :, 2 * u : 2 * u + 2, :])
+                wear_sb[g, 2 * u] = pair[:, 0, :]
+                wear_sb[g, 2 * u + 1] = pair[:, 1, :]
+
+        w2_codes = keep.tile([P, passes * H], I32, name="w2_codes", align_bytes=64)
+        nc.vector.tensor_copy(
+            out=w2_codes[:].rearrange("p (a t m) -> p a m t", a=passes, t=PACK),
+            in_=w2_raw[:].rearrange("p a (m t) -> p a m t", t=PACK),
+        )
+        w4_codes = keep.tile([P, 2 * N], U8, name="w4_codes", align_bytes=64)
+        nc.vector.tensor_copy(
+            out=w4_codes[:].rearrange("p (g t m b) -> p g m t b", g=groups, t=PACK, b=2),
+            in_=w4_raw[:].rearrange("p (g m t b) -> p g m t b", g=groups, t=PACK, b=2),
+        )
+
+        v_codes = [
+            [keep.tile([P, BANK], U32, name="v_codes%d%d" % (a, hf), align_bytes=64) for hf in range(halves)]
+            for a in range(passes)
+        ]
+        v_plane = [keep.tile([P, BANK], U8, name="v_plane%d" % hf, align_bytes=64) for hf in range(halves)]
+        w2_plane = keep.tile([P, H], U8, name="w2_plane", align_bytes=64)
+
+        def look_up(out, window, hf):
+            entries = slice(hf * BANK // LIST_ROWS, (hf + 1) * BANK // LIST_ROWS)
+            nc.vector.tensor_copy(out[hf][:], window.indirect(idx[:, entries]))
+
+        look_up(v_codes[0], tab[0][:].bitcast(U32), 0)
+        nc.vector.tensor_copy(
+            out=w2_plane[:].rearrange("p (t m) -> p m t", t=PACK),
+            in_=w2_plane_raw[:].rearrange("p (m t) -> p m t", t=PACK),
+        )
+        look_up(v_plane, tab_plane[:], 0)
+        look_up(v_codes[0], tab[0][:].bitcast(U32), 1)
+        look_up(v_plane, tab_plane[:], 1)
+        for hf in range(halves):
+            look_up(v_codes[1], tab[1][:].bitcast(U32), hf)
+
+        def product(codes, planes, t, hf, banks):
+            acc = psum.tile([P, BANK], F32, name="acc", tag=banks)
+            for a in range(passes):
+                nc.tensor.matmul_mx(
+                    out=acc[:],
+                    lhsT=codes[a][:, t * P : (t + 1) * P].bitcast(FP8X4),
+                    lhsT_scale=planes[a][:, t * P : (t + 1) * P],
+                    rhs=v_codes[a][hf][:].bitcast(FP8X4),
+                    rhs_scale=v_plane[hf][4 * a : P, :],
+                    start=(a == 0),
+                    stop=(a == passes - 1),
+                )
+            return acc
+
+        def round_weight(name, a, copy):
+            if name == "w1":
+                rounded = keep.tile([P, PACK * H], BF16, name="rounded", tag="tab%d" % (1 - a), align_bytes=64)
+            else:
+                rounded = wide.tile([P, PACK * H], BF16, name="rounded", tag="bf16x4", align_bytes=64)
+            copy(
+                out=rounded[:].rearrange("p (t m i) -> p m i t", t=PACK, i=PACK),
+                in_=raw[name, a][:].rearrange("p i (m t) -> p m i t", t=PACK),
+            )
+            return rounded
+
+        def quantize(rounded, name):
+            width = rounded.shape[1] // PACK
+            codes = keep.tile([P, width], U32, name=name + "_codes", align_bytes=64)
+            plane = keep.tile([P, width], U8, name=name + "_plane", align_bytes=64)
+            nc.vector.quantize_mx(out=codes[:].bitcast(FP8X4), scales=plane[:], in_=rounded[:])
+            return codes, plane
+
+        def interleave(copy, out, in_):
+            copy(
+                out=out.rearrange("p (c i t) -> p c t i", i=4, t=PACK),
+                in_=in_.rearrange("p t (c i) -> p c t i", i=4),
+            )
+
+        slices = [(hf, t) for hf in range(halves) for t in range(PACK)]
+
+        w2_c = [w2_codes[:, a * H : (a + 1) * H] for a in range(passes)]
+        w2_p = [w2_plane[4 * a : P, :] for a in range(passes)]
+        resp = {}
+        for hf, t in slices:
+            acc = product(w2_c, w2_p, t, hf, "packed")
+            resp[hf, t] = keep.tile([P, BANK], F32, name="resp%d%d" % (hf, t))
+            nc.scalar.copy(out=resp[hf, t][:], in_=acc[:])
+
+        w1_q = [quantize(round_weight("w1", a, nc.vector.tensor_copy), "w1_%d" % a) for a in range(passes)]
+        w3_r = [round_weight("w3", a, nc.scalar.copy) for a in range(passes)]
+        for hf, t in slices:
+            acc = product([q[0][:] for q in w1_q], [q[1][:] for q in w1_q], t, hf, "made")
+            nc.vector.tensor_tensor(resp[hf, t][:], acc[:], resp[hf, t][:], ALU.min)
+        w3_q = [quantize(w3_r[a], "w3_%d" % a) for a in range(passes)]
+        h_rows = [wide.tile([P, PACK, BANK], BF16, name="h_rows", tag="bf16x4", align_bytes=64) for hf in range(halves)]
+        h_rounded = []
+        h_q = []
+        for hf, t in slices:
+            if (hf, t) == slices[-1]:
+                w4_plane = keep.tile([P, N], U8, name="w4_plane", align_bytes=64)
+                nc.vector.tensor_copy(
+                    out=w4_plane[:].rearrange("p (g t m) -> p g m t", g=groups, t=PACK),
+                    in_=w4_plane_raw[:].rearrange("p (g m t) -> p g m t", g=groups, t=PACK),
+                )
+                h_q.append(quantize(h_rounded[0], "h0"))
+            acc = product([q[0][:] for q in w3_q], [q[1][:] for q in w3_q], t, hf, "made")
+            nc.vector.tensor_tensor(resp[hf, t][:], acc[:], resp[hf, t][:], ALU.max)
+            nc.scalar.activation(h_rows[hf][:, t, :], resp[hf, t][:], ACT.Copy, scale=gh_sb[:, t : t + 1])
+            if t == PACK - 1:
+                woven = wide.tile([P, PACK * BANK], BF16, name="woven", tag="bf16x4", align_bytes=64)
+                interleave(nc.scalar.copy, woven[:], h_rows[hf][:])
+                h_rounded.append(woven)
+
+        rows = [(g, t) for g in range(groups) for t in range(PACK)]
+        feat = {gt: keep.tile([P, S], F32, name="feat%d%d" % gt) for gt in rows}
+
+        def features(g, t, hf):
+            acc = psum.tile([P, BANK], F32, name="acc", tag="packed")
+            first = (g * PACK + t) * P
+            cols = slice(hf * BANK, (hf + 1) * BANK)
+            nc.tensor.matmul_mx(
+                out=acc[:],
+                lhsT=w4_codes[:, 2 * first : 2 * (first + P)].bitcast(FP4X4),
+                lhsT_scale=w4_plane[:, first : first + P],
+                rhs=h_q[hf][0][:].bitcast(FP8X4),
+                rhs_scale=h_q[hf][1][:],
+                start=True,
+                stop=True,
+            )
+            nc.vector.tensor_tensor(feat[g, t][:, cols], acc[:], wear_sb[g, t][:, cols], ALU.mult)
+
+        for n, (g, t) in enumerate(rows):
+            features(g, t, 0)
+            if n == PACK:
+                h_q.append(quantize(h_rounded[1], "h1"))
+
+        y_rows = out_0.rearrange("(g p t) m -> g p t m", g=groups, t=PACK)
+        steps = [(0, t, 0, M) for t in range(PACK)]
+        steps += [(1, t, m0, m0 + M // 2) for m0 in (0, M // 2) for t in range(PACK)]
+        todo = list(rows)
+        features(*todo.pop(0), 1)
+        y = {}
+        for g, t, m0, m1 in steps:
+            width = m1 - m0
+            entries = slice(m0 // LIST_ROWS, m1 // LIST_ROWS)
+            if t == 0:
+                y[g, m0] = wide.tile([P, PACK, width], F32, name="y", tag="f32x4")
+            picked = ring.tile([P, width], F32, name="picked", tag="picked")
+            nc.vector.tensor_copy(picked[:], feat[g, t][:].indirect(left[:, entries]))
+            if todo:
+                features(*todo.pop(0), 1)
+            pair_sum = ring.tile([P, width], F32, name="pair_sum", tag="pair_sum")
+            nc.vector.tensor_tensor(pair_sum[:], feat[g, t][:].indirect(right[:, entries]), picked[:], ALU.add)
+            nc.scalar.activation(pair_sum[:], pair_sum[:], ACT.Tanh)
+            nc.scalar.activation(y[g, m0][:, t, :], pair_sum[:], ACT.Copy, scale=gy_sb[:, g, t : t + 1])
+            nc.sync.dma_start(out=y_rows[g, :, t, m0:m1], in_=y[g, m0][:, t, :])
+            if t == PACK - 1:
+                woven = wide.tile([P, PACK * width], BF16, name="woven", tag="bf16x4", align_bytes=64)
+                last = (g, m1) == (groups - 1, M)
+                interleave(nc.vector.tensor_copy if last else nc.scalar.copy, woven[:], y[g, m0][:])
+                codes, plane = quantize(woven, "y%d_%d" % (g, m0))
+                nc.sync.dma_start(
+                    out=out_1[g, :, m0:m1, :].rearrange("p m i -> p (m i)").bitcast(I32), in_=codes[:].bitcast(I32)
+                )
+                for q in range(QUADS):
+                    queue = nc.scalar if last and q % 2 else nc.sync
+                    queue.dma_start(
+                        out=out_2[g, 4 * q : 4 * q + 4, m0:m1].bitcast(I32),
+                        in_=plane[32 * q : 32 * q + 4, :].bitcast(I32),
+                    )

@@ -42,13 +42,10 @@ def tile_list_zipper_tooth_features_kernel(
         tab_plane = keep.tile([P, T], U8, name="tab_plane", align_bytes=64)
         w2_plane_raw = keep.tile([P, H], U8, name="w2_plane_raw", align_bytes=64)
         w4_plane_raw = keep.tile([P, N], U8, name="w4_plane_raw", align_bytes=64)
-        for plane in (w2_plane_raw, tab_plane, w4_plane_raw):
+        nc.gpsimd.memset(tab_plane[:].bitcast(I32), 0)
+        for plane in (w2_plane_raw, w4_plane_raw):
             nc.vector.memset(plane[:].bitcast(I32), 0)
 
-        w2_raw = keep.tile([P, passes, H], I32, name="w2_raw")
-        nc.sync.dma_start(out=w2_raw[:], in_=w2_words.rearrange("a p c i -> p a (c i)").bitcast(I32))
-        w4_raw = keep.tile([P, 2 * N], U8, name="w4_raw")
-        nc.sync.dma_start(out=w4_raw[:].bitcast(I32), in_=w4_words[0].bitcast(I32))
         idx = keep.tile([P, S // LIST_ROWS], U16, name="idx")
         nc.sync.dma_start(idx[:], offs)
         left = keep.tile([P, M // LIST_ROWS], U16, name="left")
@@ -59,20 +56,25 @@ def tile_list_zipper_tooth_features_kernel(
         nc.sync.dma_start(out=gh_sb[:], in_=gh.rearrange("(p t) -> p t", t=PACK))
         gy_sb = keep.tile([P, groups, PACK], F32, name="gy_sb")
         nc.sync.dma_start(out=gy_sb[:], in_=gy.rearrange("(g p t) -> p g t", g=groups, t=PACK))
+        w2_raw = keep.tile([P, passes, H], I32, name="w2_raw")
+        nc.sync.dma_start(out=w2_raw[:], in_=w2_words.rearrange("a p c i -> p a (c i)").bitcast(I32))
+        w4_raw = keep.tile([P, 2 * N], U8, name="w4_raw")
+        nc.sync.dma_start(out=w4_raw[:].bitcast(I32), in_=w4_words[0].bitcast(I32))
 
         tab = [keep.tile([P, T], I32, name="tab%d" % a, tag="tab%d" % a, align_bytes=64) for a in range(passes)]
-        nc.sync.dma_start(out=tab[0][:], in_=tab_words[0].rearrange("p t i -> p (t i)").bitcast(I32))
+        tab_src = [tab_words[a].rearrange("p t i -> p (t i)").bitcast(I32) for a in range(passes)]
+        nc.sync.dma_start(out=tab[0][:], in_=tab_src[0])
         for q in range(QUADS):
-            nc.scalar.dma_start(
-                out=w2_plane_raw[32 * q : 32 * q + 4 * passes, :].bitcast(I32),
-                in_=w2_scales[:, 4 * q : 4 * q + 4, :].bitcast(I32),
-            )
-        for q in range(QUADS):
-            nc.scalar.dma_start(
+            nc.gpsimd.dma_start(
                 out=tab_plane[32 * q : 32 * q + 4 * passes, :].bitcast(I32),
                 in_=tab_scales[:, 4 * q : 4 * q + 4, :].bitcast(I32),
             )
-        nc.sync.dma_start(out=tab[1][:], in_=tab_words[1].rearrange("p t i -> p (t i)").bitcast(I32))
+        for q in range(QUADS):
+            nc.sync.dma_start(
+                out=w2_plane_raw[32 * q : 32 * q + 4 * passes, :].bitcast(I32),
+                in_=w2_scales[:, 4 * q : 4 * q + 4, :].bitcast(I32),
+            )
+        nc.sync.dma_start(out=tab[1][:], in_=tab_src[1])
 
         raw = {}
         for name, w in (("w1", w1), ("w3", w3)):
@@ -117,14 +119,14 @@ def tile_list_zipper_tooth_features_kernel(
             entries = slice(hf * BANK // LIST_ROWS, (hf + 1) * BANK // LIST_ROWS)
             nc.vector.tensor_copy(out[hf][:], window.indirect(idx[:, entries]))
 
-        look_up(v_codes[0], tab[0][:].bitcast(U32), 0)
         nc.vector.tensor_copy(
             out=w2_plane[:].rearrange("p (t m) -> p m t", t=PACK),
             in_=w2_plane_raw[:].rearrange("p (m t) -> p m t", t=PACK),
         )
-        look_up(v_plane, tab_plane[:], 0)
-        look_up(v_codes[0], tab[0][:].bitcast(U32), 1)
-        look_up(v_plane, tab_plane[:], 1)
+        for hf in range(halves):
+            look_up(v_plane, tab_plane[:], hf)
+        for hf in range(halves):
+            look_up(v_codes[0], tab[0][:].bitcast(U32), hf)
         for hf in range(halves):
             look_up(v_codes[1], tab[1][:].bitcast(U32), hf)
 
@@ -227,18 +229,26 @@ def tile_list_zipper_tooth_features_kernel(
         y_rows = out_0.rearrange("(g p t) m -> g p t m", g=groups, t=PACK)
         steps = [(0, t, 0, M) for t in range(PACK)]
         steps += [(1, t, m0, m0 + M // 2) for m0 in (0, M // 2) for t in range(PACK)]
-        todo = list(rows)
-        features(*todo.pop(0), 1)
+
+        def pick_left(g, t, m0, m1):
+            picked = ring.tile([P, m1 - m0], F32, name="picked", tag="picked")
+            nc.vector.tensor_copy(picked[:], feat[g, t][:].indirect(left[:, m0 // LIST_ROWS : m1 // LIST_ROWS]))
+            return picked
+
+        features(*rows[0], 1)
+        features(*rows[1], 1)
+        ahead = pick_left(*steps[0])
         y = {}
-        for g, t, m0, m1 in steps:
+        for n, (g, t, m0, m1) in enumerate(steps):
             width = m1 - m0
             entries = slice(m0 // LIST_ROWS, m1 // LIST_ROWS)
             if t == 0:
                 y[g, m0] = wide.tile([P, PACK, width], F32, name="y", tag="f32x4")
-            picked = ring.tile([P, width], F32, name="picked", tag="picked")
-            nc.vector.tensor_copy(picked[:], feat[g, t][:].indirect(left[:, entries]))
-            if todo:
-                features(*todo.pop(0), 1)
+            picked = ahead
+            if n + 2 < len(rows):
+                features(*rows[n + 2], 1)
+            if n + 1 < len(steps):
+                ahead = pick_left(*steps[n + 1])
             pair_sum = ring.tile([P, width], F32, name="pair_sum", tag="pair_sum")
             nc.vector.tensor_tensor(pair_sum[:], feat[g, t][:].indirect(right[:, entries]), picked[:], ALU.add)
             nc.scalar.activation(pair_sum[:], pair_sum[:], ACT.Tanh)

@@ -42,8 +42,7 @@ def tile_list_zipper_tooth_features_kernel(
         tab_plane = keep.tile([P, T], U8, name="tab_plane", align_bytes=64)
         w2_plane_raw = keep.tile([P, H], U8, name="w2_plane_raw", align_bytes=64)
         w4_plane_raw = keep.tile([P, N], U8, name="w4_plane_raw", align_bytes=64)
-        nc.gpsimd.memset(tab_plane[:].bitcast(I32), 0)
-        for plane in (w2_plane_raw, w4_plane_raw):
+        for plane in (tab_plane, w2_plane_raw, w4_plane_raw):
             nc.vector.memset(plane[:].bitcast(I32), 0)
 
         idx = keep.tile([P, S // LIST_ROWS], U16, name="idx")
@@ -63,13 +62,15 @@ def tile_list_zipper_tooth_features_kernel(
 
         tab = [keep.tile([P, T], I32, name="tab%d" % a, tag="tab%d" % a, align_bytes=64) for a in range(passes)]
         tab_src = [tab_words[a].rearrange("p t i -> p (t i)").bitcast(I32) for a in range(passes)]
-        nc.sync.dma_start(out=tab[0][:], in_=tab_src[0])
+        nc.sync.dma_start(out=tab[0][:, : T // 2], in_=tab_src[0][:, : T // 2])
         for q in range(QUADS):
-            nc.gpsimd.dma_start(
+            nc.sync.dma_start(
                 out=tab_plane[32 * q : 32 * q + 4 * passes, :].bitcast(I32),
                 in_=tab_scales[:, 4 * q : 4 * q + 4, :].bitcast(I32),
             )
         for q in range(QUADS):
+            if q == 2:
+                nc.sync.dma_start(out=tab[0][:, T // 2 :], in_=tab_src[0][:, T // 2 :])
             nc.sync.dma_start(
                 out=w2_plane_raw[32 * q : 32 * q + 4 * passes, :].bitcast(I32),
                 in_=w2_scales[:, 4 * q : 4 * q + 4, :].bitcast(I32),
@@ -119,14 +120,14 @@ def tile_list_zipper_tooth_features_kernel(
             entries = slice(hf * BANK // LIST_ROWS, (hf + 1) * BANK // LIST_ROWS)
             nc.vector.tensor_copy(out[hf][:], window.indirect(idx[:, entries]))
 
+        for hf in range(halves):
+            look_up(v_plane, tab_plane[:], hf)
+        look_up(v_codes[0], tab[0][:].bitcast(U32), 0)
         nc.vector.tensor_copy(
             out=w2_plane[:].rearrange("p (t m) -> p m t", t=PACK),
             in_=w2_plane_raw[:].rearrange("p (m t) -> p m t", t=PACK),
         )
-        for hf in range(halves):
-            look_up(v_plane, tab_plane[:], hf)
-        for hf in range(halves):
-            look_up(v_codes[0], tab[0][:].bitcast(U32), hf)
+        look_up(v_codes[0], tab[0][:].bitcast(U32), 1)
         for hf in range(halves):
             look_up(v_codes[1], tab[1][:].bitcast(U32), hf)
 
@@ -206,7 +207,7 @@ def tile_list_zipper_tooth_features_kernel(
         rows = [(g, t) for g in range(groups) for t in range(PACK)]
         feat = {gt: keep.tile([P, S], F32, name="feat%d%d" % gt) for gt in rows}
 
-        def features(g, t, hf):
+        def features(g, t, hf, on_vector=True):
             acc = psum.tile([P, BANK], F32, name="acc", tag="packed")
             first = (g * PACK + t) * P
             cols = slice(hf * BANK, (hf + 1) * BANK)
@@ -219,7 +220,11 @@ def tile_list_zipper_tooth_features_kernel(
                 start=True,
                 stop=True,
             )
-            nc.vector.tensor_tensor(feat[g, t][:, cols], acc[:], wear_sb[g, t][:, cols], ALU.mult)
+            if on_vector:
+                nc.vector.tensor_tensor(feat[g, t][:, cols], acc[:], wear_sb[g, t][:, cols], ALU.mult)
+            else:
+                nc.scalar.copy(out=feat[g, t][:, cols], in_=acc[:])
+                nc.gpsimd.tensor_tensor(feat[g, t][:, cols], feat[g, t][:, cols], wear_sb[g, t][:, cols], ALU.mult)
 
         for n, (g, t) in enumerate(rows):
             features(g, t, 0)
@@ -230,41 +235,49 @@ def tile_list_zipper_tooth_features_kernel(
         steps = [(0, t, 0, M) for t in range(PACK)]
         steps += [(1, t, m0, m0 + M // 2) for m0 in (0, M // 2) for t in range(PACK)]
 
-        def pick_left(g, t, m0, m1):
-            picked = ring.tile([P, m1 - m0], F32, name="picked", tag="picked")
-            nc.vector.tensor_copy(picked[:], feat[g, t][:].indirect(left[:, m0 // LIST_ROWS : m1 // LIST_ROWS]))
-            return picked
+        picked = {}
+
+        def pick_left(g, t):
+            picked[g, t] = wide.tile([P, M], F32, name="picked", tag="picked", bufs=5)
+            nc.vector.tensor_copy(picked[g, t][:], feat[g, t][:].indirect(left[:]))
 
         features(*rows[0], 1)
         features(*rows[1], 1)
-        ahead = pick_left(*steps[0])
+        features(*rows[2], 1, on_vector=False)
+        pick_left(*rows[0])
         y = {}
+        y_codes = [keep.tile([P, M], U32, name="y_codes%d" % g, align_bytes=64) for g in range(groups)]
+        y_plane = [keep.tile([P, M], U8, name="y_plane%d" % g, align_bytes=64) for g in range(groups)]
         for n, (g, t, m0, m1) in enumerate(steps):
             width = m1 - m0
             entries = slice(m0 // LIST_ROWS, m1 // LIST_ROWS)
             if t == 0:
                 y[g, m0] = wide.tile([P, PACK, width], F32, name="y", tag="f32x4")
-            picked = ahead
-            if n + 2 < len(rows):
-                features(*rows[n + 2], 1)
-            if n + 1 < len(steps):
-                ahead = pick_left(*steps[n + 1])
+            if n + 3 < len(rows):
+                features(*rows[n + 3], 1, on_vector=False)
+            if n + 1 < len(rows):
+                pick_left(*rows[n + 1])
             pair_sum = ring.tile([P, width], F32, name="pair_sum", tag="pair_sum")
-            nc.vector.tensor_tensor(pair_sum[:], feat[g, t][:].indirect(right[:, entries]), picked[:], ALU.add)
+            nc.vector.tensor_tensor(pair_sum[:], feat[g, t][:].indirect(right[:, entries]), picked[g, t][:, m0:m1], ALU.add)
             nc.scalar.activation(pair_sum[:], pair_sum[:], ACT.Tanh)
             nc.scalar.activation(y[g, m0][:, t, :], pair_sum[:], ACT.Copy, scale=gy_sb[:, g, t : t + 1])
-            nc.sync.dma_start(out=y_rows[g, :, t, m0:m1], in_=y[g, m0][:, t, :])
+            if t % 2:
+                nc.sync.dma_start(out=y_rows[g, :, t - 1 : t + 1, m0:m1], in_=y[g, m0][:, t - 1 : t + 1, :])
             if t == PACK - 1:
                 woven = wide.tile([P, PACK * width], BF16, name="woven", tag="bf16x4", align_bytes=64)
                 last = (g, m1) == (groups - 1, M)
                 interleave(nc.vector.tensor_copy if last else nc.scalar.copy, woven[:], y[g, m0][:])
-                codes, plane = quantize(woven, "y%d_%d" % (g, m0))
-                nc.sync.dma_start(
-                    out=out_1[g, :, m0:m1, :].rearrange("p m i -> p (m i)").bitcast(I32), in_=codes[:].bitcast(I32)
+                nc.vector.quantize_mx(
+                    out=y_codes[g][:, m0:m1].bitcast(FP8X4), scales=y_plane[g][:, m0:m1], in_=woven[:]
                 )
-                for q in range(QUADS):
-                    queue = nc.scalar if last and q % 2 else nc.sync
-                    queue.dma_start(
-                        out=out_2[g, 4 * q : 4 * q + 4, m0:m1].bitcast(I32),
-                        in_=plane[32 * q : 32 * q + 4, :].bitcast(I32),
-                    )
+                nc.sync.dma_start(
+                    out=out_1[g, :, m0:m1, :].rearrange("p m i -> p (m i)").bitcast(I32),
+                    in_=y_codes[g][:, m0:m1].bitcast(I32),
+                )
+                if m1 == M:
+                    for q in range(QUADS):
+                        queue = nc.scalar if last and q % 2 else nc.sync
+                        queue.dma_start(
+                            out=out_2[g, 4 * q : 4 * q + 4, :].bitcast(I32),
+                            in_=y_plane[g][32 * q : 32 * q + 4, :].bitcast(I32),
+                        )

@@ -22,6 +22,10 @@ PASS = P * PACK
 BANK = 512
 LIST_ROWS = 16
 QUADS = 4
+QUAD = P // QUADS
+PLANE_ROWS = 4
+LINE = 4
+MX_ALIGN = 64
 
 
 def tile_list_zipper_tooth_features_kernel(
@@ -33,15 +37,28 @@ def tile_list_zipper_tooth_features_kernel(
     halves = S // BANK
     groups = N // PASS
 
+    def words(dram):
+        return dram.rearrange("p c i -> p (c i)").bitcast(I32)
+
+    def quadrant_rows(plane, q, count):
+        return plane[QUAD * q : QUAD * q + count, :].bitcast(I32)
+
+    def scale_rows(q):
+        return slice(PLANE_ROWS * q, PLANE_ROWS * (q + 1))
+
+    def entries(first, last):
+        return slice(first // LIST_ROWS, last // LIST_ROWS)
+
     with ExitStack() as ctx:
         keep = ctx.enter_context(tc.tile_pool(name="keep", bufs=1))
         wide = ctx.enter_context(tc.tile_pool(name="wide", bufs=4))
         ring = ctx.enter_context(tc.tile_pool(name="ring", bufs=3))
-        psum = ctx.enter_context(tc.psum_pool(name="psum", bufs=4))
+        psum = ctx.enter_context(tc.psum_pool(name="psum", bufs=PACK))
+        bank_sets = ("low", "high")
 
-        tab_plane = keep.tile([P, T], U8, name="tab_plane", align_bytes=64)
-        w2_plane_raw = keep.tile([P, H], U8, name="w2_plane_raw", align_bytes=64)
-        w4_plane_raw = keep.tile([P, N], U8, name="w4_plane_raw", align_bytes=64)
+        tab_plane = keep.tile([P, T], U8, name="tab_plane", align_bytes=MX_ALIGN)
+        w2_plane_raw = keep.tile([P, H], U8, name="w2_plane_raw", align_bytes=MX_ALIGN)
+        w4_plane_raw = keep.tile([P, N], U8, name="w4_plane_raw", align_bytes=MX_ALIGN)
         for plane in (tab_plane, w2_plane_raw, w4_plane_raw):
             nc.vector.memset(plane[:].bitcast(I32), 0)
 
@@ -55,229 +72,221 @@ def tile_list_zipper_tooth_features_kernel(
         nc.sync.dma_start(out=gh_sb[:], in_=gh.rearrange("(p t) -> p t", t=PACK))
         gy_sb = keep.tile([P, groups, PACK], F32, name="gy_sb")
         nc.sync.dma_start(out=gy_sb[:], in_=gy.rearrange("(g p t) -> p g t", g=groups, t=PACK))
-        w2_raw = keep.tile([P, passes, H], I32, name="w2_raw")
-        nc.sync.dma_start(out=w2_raw[:], in_=w2_words.rearrange("a p c i -> p a (c i)").bitcast(I32))
-        w4_raw = keep.tile([P, 2 * N], U8, name="w4_raw")
+        w2_raw = [keep.tile([P, H], I32, name="w2_raw%d" % a) for a in range(passes)]
+        for a in range(passes):
+            nc.sync.dma_start(out=w2_raw[a][:], in_=words(w2_words[a]))
+
+        tab = [keep.tile([P, T], I32, name="tab%d" % a, tag="tab%d" % a, align_bytes=MX_ALIGN) for a in range(passes)]
+        nc.sync.dma_start(out=tab[0][:, : T // 2], in_=words(tab_words[0])[:, : T // 2])
+        for q in range(QUADS):
+            nc.sync.dma_start(
+                out=quadrant_rows(tab_plane, q, PLANE_ROWS * passes), in_=tab_scales[:, scale_rows(q), :].bitcast(I32)
+            )
+        for q in range(QUADS):
+            if q == QUADS // 2:
+                nc.sync.dma_start(out=tab[0][:, T // 2 :], in_=words(tab_words[0])[:, T // 2 :])
+            nc.sync.dma_start(
+                out=quadrant_rows(w2_plane_raw, q, PLANE_ROWS * passes), in_=w2_scales[:, scale_rows(q), :].bitcast(I32)
+            )
+        nc.sync.dma_start(out=tab[1][:], in_=words(tab_words[1]))
+
+        def load_weight(pool, w, a, first, last, tag):
+            raw = pool.tile([P, PACK, last - first], F32, name="raw", tag=tag)
+            nc.sync.dma_start(
+                out=raw[:], in_=w[a * PASS : (a + 1) * PASS, first:last].rearrange("(p i) c -> p i c", i=PACK)
+            )
+            return raw, first, last
+
+        w1_raw = [
+            [load_weight(keep, w1, 0, 0, H, "w1_raw0")],
+            [load_weight(keep, w1, 1, c, c + H // 2, "w1_raw1_%d" % c) for c in (0, H // 2)],
+        ]
+        w3_raw = [[load_weight(wide, w3, a, 0, H, "f32x4")] for a in range(passes)]
+        for q in range(QUADS):
+            nc.sync.dma_start(
+                out=quadrant_rows(w4_plane_raw, q, PLANE_ROWS), in_=w4_scales[0, scale_rows(q), :].bitcast(I32)
+            )
+        w4_raw = keep.tile([P, N], U16, name="w4_raw")
         nc.sync.dma_start(out=w4_raw[:].bitcast(I32), in_=w4_words[0].bitcast(I32))
-
-        tab = [keep.tile([P, T], I32, name="tab%d" % a, tag="tab%d" % a, align_bytes=64) for a in range(passes)]
-        tab_src = [tab_words[a].rearrange("p t i -> p (t i)").bitcast(I32) for a in range(passes)]
-        nc.sync.dma_start(out=tab[0][:, : T // 2], in_=tab_src[0][:, : T // 2])
-        for q in range(QUADS):
-            nc.sync.dma_start(
-                out=tab_plane[32 * q : 32 * q + 4 * passes, :].bitcast(I32),
-                in_=tab_scales[:, 4 * q : 4 * q + 4, :].bitcast(I32),
-            )
-        for q in range(QUADS):
-            if q == 2:
-                nc.sync.dma_start(out=tab[0][:, T // 2 :], in_=tab_src[0][:, T // 2 :])
-            nc.sync.dma_start(
-                out=w2_plane_raw[32 * q : 32 * q + 4 * passes, :].bitcast(I32),
-                in_=w2_scales[:, 4 * q : 4 * q + 4, :].bitcast(I32),
-            )
-        nc.sync.dma_start(out=tab[1][:], in_=tab_src[1])
-
-        raw = {}
-        for name, w in (("w1", w1), ("w3", w3)):
-            for a in range(passes):
-                raw[name, a] = wide.tile([P, PACK, H], F32, name="raw", tag="f32x4")
-                nc.sync.dma_start(
-                    out=raw[name, a][:], in_=w[a * PASS : (a + 1) * PASS, :].rearrange("(p i) c -> p i c", i=PACK)
-                )
-        for q in range(QUADS):
-            nc.sync.dma_start(
-                out=w4_plane_raw[32 * q : 32 * q + 4, :].bitcast(I32),
-                in_=w4_scales[0, 4 * q : 4 * q + 4, :].bitcast(I32),
-            )
         wear_rows = wear.rearrange("(g p t) j -> g p t j", g=groups, t=PACK)
         wear_sb = {}
         for g in range(groups):
-            for u in range(2):
-                pair = keep.tile([P, 2, S], F32, name="wear%d%d" % (g, u))
-                nc.sync.dma_start(out=pair[:], in_=wear_rows[g, :, 2 * u : 2 * u + 2, :])
-                wear_sb[g, 2 * u] = pair[:, 0, :]
-                wear_sb[g, 2 * u + 1] = pair[:, 1, :]
+            for t in range(0, PACK, 2):
+                two_slices = keep.tile([P, 2, S], F32, name="wear%d%d" % (g, t))
+                nc.sync.dma_start(out=two_slices[:], in_=wear_rows[g, :, t : t + 2, :])
+                wear_sb[g, t] = two_slices[:, 0, :]
+                wear_sb[g, t + 1] = two_slices[:, 1, :]
 
-        w2_codes = keep.tile([P, passes * H], I32, name="w2_codes", align_bytes=64)
-        nc.vector.tensor_copy(
-            out=w2_codes[:].rearrange("p (a t m) -> p a m t", a=passes, t=PACK),
-            in_=w2_raw[:].rearrange("p a (m t) -> p a m t", t=PACK),
-        )
-        w4_codes = keep.tile([P, 2 * N], U8, name="w4_codes", align_bytes=64)
-        nc.vector.tensor_copy(
-            out=w4_codes[:].rearrange("p (g t m b) -> p g m t b", g=groups, t=PACK, b=2),
-            in_=w4_raw[:].rearrange("p (g m t b) -> p g m t b", g=groups, t=PACK, b=2),
-        )
+        def deal(out, in_):
+            nc.vector.tensor_copy(
+                out=out.rearrange("p (g t m) -> p g m t", t=PACK, m=P),
+                in_=in_.rearrange("p (g m t) -> p g m t", t=PACK, m=P),
+            )
+
+        def round_weight(rounded, pieces, copy):
+            dealt = rounded[:].rearrange("p (t m i) -> p m i t", t=PACK, i=PACK)
+            for raw, first, last in pieces:
+                copy(out=dealt[:, first // PACK : last // PACK], in_=raw[:].rearrange("p i (m t) -> p m i t", t=PACK))
+            return rounded
+
+        def weave(copy, slices_in):
+            woven = wide.tile([P, PACK * slices_in.shape[2]], BF16, name="woven", tag="bf16x4", align_bytes=MX_ALIGN)
+            copy(
+                out=woven[:].rearrange("p (c i t) -> p c t i", i=LINE, t=PACK),
+                in_=slices_in.rearrange("p t (c i) -> p c t i", i=LINE),
+            )
+            return woven
+
+        def quantize(rounded, name):
+            width = rounded.shape[1] // PACK
+            codes = keep.tile([P, width], U32, name=name + "_codes", align_bytes=MX_ALIGN)
+            plane = keep.tile([P, width], U8, name=name + "_plane", align_bytes=MX_ALIGN)
+            nc.vector.quantize_mx(out=codes[:].bitcast(FP8X4), scales=plane[:], in_=rounded[:])
+            return codes[:], plane[:]
+
+        w2_codes = [keep.tile([P, H], I32, name="w2_codes%d" % a, align_bytes=MX_ALIGN) for a in range(passes)]
+        for a in range(passes):
+            deal(w2_codes[a][:], w2_raw[a][:])
 
         v_codes = [
-            [keep.tile([P, BANK], U32, name="v_codes%d%d" % (a, hf), align_bytes=64) for hf in range(halves)]
+            [keep.tile([P, BANK], U32, name="v_codes%d%d" % (a, hf), align_bytes=MX_ALIGN) for hf in range(halves)]
             for a in range(passes)
         ]
-        v_plane = [keep.tile([P, BANK], U8, name="v_plane%d" % hf, align_bytes=64) for hf in range(halves)]
-        w2_plane = keep.tile([P, H], U8, name="w2_plane", align_bytes=64)
+        v_plane = [keep.tile([P, BANK], U8, name="v_plane%d" % hf, align_bytes=MX_ALIGN) for hf in range(halves)]
+        w2_plane = keep.tile([P, H], U8, name="w2_plane", align_bytes=MX_ALIGN)
 
         def look_up(out, window, hf):
-            entries = slice(hf * BANK // LIST_ROWS, (hf + 1) * BANK // LIST_ROWS)
-            nc.vector.tensor_copy(out[hf][:], window.indirect(idx[:, entries]))
+            nc.vector.tensor_copy(out[hf][:], window.indirect(idx[:, entries(hf * BANK, (hf + 1) * BANK)]))
 
         for hf in range(halves):
             look_up(v_plane, tab_plane[:], hf)
         look_up(v_codes[0], tab[0][:].bitcast(U32), 0)
-        nc.vector.tensor_copy(
-            out=w2_plane[:].rearrange("p (t m) -> p m t", t=PACK),
-            in_=w2_plane_raw[:].rearrange("p (m t) -> p m t", t=PACK),
-        )
+        deal(w2_plane[:], w2_plane_raw[:])
         look_up(v_codes[0], tab[0][:].bitcast(U32), 1)
         for hf in range(halves):
             look_up(v_codes[1], tab[1][:].bitcast(U32), hf)
 
-        def product(codes, planes, t, hf, banks):
+        def response(weight, t, hf, banks):
             acc = psum.tile([P, BANK], F32, name="acc", tag=banks)
-            for a in range(passes):
+            for a, (codes, plane) in enumerate(weight):
                 nc.tensor.matmul_mx(
                     out=acc[:],
-                    lhsT=codes[a][:, t * P : (t + 1) * P].bitcast(FP8X4),
-                    lhsT_scale=planes[a][:, t * P : (t + 1) * P],
+                    lhsT=codes[:, t * P : (t + 1) * P].bitcast(FP8X4),
+                    lhsT_scale=plane[:, t * P : (t + 1) * P],
                     rhs=v_codes[a][hf][:].bitcast(FP8X4),
-                    rhs_scale=v_plane[hf][4 * a : P, :],
+                    rhs_scale=v_plane[hf][PLANE_ROWS * a : P, :],
                     start=(a == 0),
                     stop=(a == passes - 1),
                 )
             return acc
 
-        def round_weight(name, a, copy):
-            if name == "w1":
-                rounded = keep.tile([P, PACK * H], BF16, name="rounded", tag="tab%d" % (1 - a), align_bytes=64)
-            else:
-                rounded = wide.tile([P, PACK * H], BF16, name="rounded", tag="bf16x4", align_bytes=64)
-            copy(
-                out=rounded[:].rearrange("p (t m i) -> p m i t", t=PACK, i=PACK),
-                in_=raw[name, a][:].rearrange("p i (m t) -> p m i t", t=PACK),
-            )
-            return rounded
+        banks_of_h = [(hf, t) for hf in range(halves) for t in range(PACK)]
 
-        def quantize(rounded, name):
-            width = rounded.shape[1] // PACK
-            codes = keep.tile([P, width], U32, name=name + "_codes", align_bytes=64)
-            plane = keep.tile([P, width], U8, name=name + "_plane", align_bytes=64)
-            nc.vector.quantize_mx(out=codes[:].bitcast(FP8X4), scales=plane[:], in_=rounded[:])
-            return codes, plane
+        w2_q = [(w2_codes[a][:], w2_plane[PLANE_ROWS * a : P, :]) for a in range(passes)]
+        joined = {}
+        for hf, t in banks_of_h:
+            acc = response(w2_q, t, hf, bank_sets[1])
+            joined[hf, t] = keep.tile([P, BANK], F32, name="joined%d%d" % (hf, t))
+            nc.scalar.copy(out=joined[hf, t][:], in_=acc[:])
 
-        def interleave(copy, out, in_):
-            copy(
-                out=out.rearrange("p (c i t) -> p c t i", i=4, t=PACK),
-                in_=in_.rearrange("p t (c i) -> p c t i", i=4),
-            )
+        w1_q = []
+        for a in range(passes):
+            rounded = keep.tile([P, PACK * H], BF16, name="rounded", tag="tab%d" % (passes - 1 - a), align_bytes=MX_ALIGN)
+            w1_q.append(quantize(round_weight(rounded, w1_raw[a], nc.vector.tensor_copy), "w1_%d" % a))
+        w3_rounded = []
+        for a in range(passes):
+            rounded = wide.tile([P, PACK * H], BF16, name="rounded", tag="bf16x4", align_bytes=MX_ALIGN)
+            w3_rounded.append(round_weight(rounded, w3_raw[a], nc.scalar.copy))
 
-        slices = [(hf, t) for hf in range(halves) for t in range(PACK)]
+        w3_q = []
+        for n, (hf, t) in enumerate(banks_of_h):
+            acc = response(w1_q, t, hf, bank_sets[hf])
+            nc.vector.tensor_tensor(joined[hf, t][:], acc[:], joined[hf, t][:], ALU.min)
+            if n == len(banks_of_h) - 3:
+                w3_q.append(quantize(w3_rounded[0], "w3_0"))
+        w3_q.append(quantize(w3_rounded[1], "w3_1"))
 
-        w2_c = [w2_codes[:, a * H : (a + 1) * H] for a in range(passes)]
-        w2_p = [w2_plane[4 * a : P, :] for a in range(passes)]
-        resp = {}
-        for hf, t in slices:
-            acc = product(w2_c, w2_p, t, hf, "packed")
-            resp[hf, t] = keep.tile([P, BANK], F32, name="resp%d%d" % (hf, t))
-            nc.scalar.copy(out=resp[hf, t][:], in_=acc[:])
-
-        w1_q = [quantize(round_weight("w1", a, nc.vector.tensor_copy), "w1_%d" % a) for a in range(passes)]
-        w3_r = [round_weight("w3", a, nc.scalar.copy) for a in range(passes)]
-        for hf, t in slices:
-            acc = product([q[0][:] for q in w1_q], [q[1][:] for q in w1_q], t, hf, "made")
-            nc.vector.tensor_tensor(resp[hf, t][:], acc[:], resp[hf, t][:], ALU.min)
-        w3_q = [quantize(w3_r[a], "w3_%d" % a) for a in range(passes)]
-        h_rows = [wide.tile([P, PACK, BANK], BF16, name="h_rows", tag="bf16x4", align_bytes=64) for hf in range(halves)]
-        h_rounded = []
+        w4_plane = [keep.tile([P, PASS], U8, name="w4_plane%d" % g, align_bytes=MX_ALIGN) for g in range(groups)]
+        w4_codes = keep.tile([P, N], U16, name="w4_codes", align_bytes=MX_ALIGN)
+        deal(w4_plane[0][:], w4_plane_raw[:, :PASS])
+        h_rows = [
+            wide.tile([P, PACK, BANK], BF16, name="h_rows", tag="bf16x4", align_bytes=MX_ALIGN) for hf in range(halves)
+        ]
+        h_woven = []
         h_q = []
-        for hf, t in slices:
-            if (hf, t) == slices[-1]:
-                w4_plane = keep.tile([P, N], U8, name="w4_plane", align_bytes=64)
-                nc.vector.tensor_copy(
-                    out=w4_plane[:].rearrange("p (g t m) -> p g m t", g=groups, t=PACK),
-                    in_=w4_plane_raw[:].rearrange("p (g m t) -> p g m t", g=groups, t=PACK),
-                )
-                h_q.append(quantize(h_rounded[0], "h0"))
-            acc = product([q[0][:] for q in w3_q], [q[1][:] for q in w3_q], t, hf, "made")
-            nc.vector.tensor_tensor(resp[hf, t][:], acc[:], resp[hf, t][:], ALU.max)
-            nc.scalar.activation(h_rows[hf][:, t, :], resp[hf, t][:], ACT.Copy, scale=gh_sb[:, t : t + 1])
+        for hf, t in banks_of_h:
+            if (hf, t) == banks_of_h[-1]:
+                deal(w4_plane[1][:], w4_plane_raw[:, PASS:])
+                deal(w4_codes[:], w4_raw[:])
+                h_q.append(quantize(h_woven[0], "h0"))
+            acc = response(w3_q, t, hf, bank_sets[hf])
+            nc.vector.tensor_tensor(joined[hf, t][:], acc[:], joined[hf, t][:], ALU.max)
+            nc.scalar.activation(h_rows[hf][:, t, :], joined[hf, t][:], ACT.Copy, scale=gh_sb[:, t : t + 1])
             if t == PACK - 1:
-                woven = wide.tile([P, PACK * BANK], BF16, name="woven", tag="bf16x4", align_bytes=64)
-                interleave(nc.scalar.copy, woven[:], h_rows[hf][:])
-                h_rounded.append(woven)
+                h_woven.append(weave(nc.scalar.copy, h_rows[hf][:]))
 
-        rows = [(g, t) for g in range(groups) for t in range(PACK)]
-        feat = {gt: keep.tile([P, S], F32, name="feat%d%d" % gt) for gt in rows}
+        slices_of_g2 = [(g, t) for g in range(groups) for t in range(PACK)]
+        g2 = {gt: keep.tile([P, S], F32, name="g2_%d%d" % gt) for gt in slices_of_g2}
 
-        def features(g, t, hf, on_vector=True):
-            acc = psum.tile([P, BANK], F32, name="acc", tag="packed")
+        def features(g, t, hf):
+            acc = psum.tile([P, BANK], F32, name="acc", tag=bank_sets[0])
             first = (g * PACK + t) * P
             cols = slice(hf * BANK, (hf + 1) * BANK)
+            codes, plane = h_q[hf]
             nc.tensor.matmul_mx(
                 out=acc[:],
-                lhsT=w4_codes[:, 2 * first : 2 * (first + P)].bitcast(FP4X4),
-                lhsT_scale=w4_plane[:, first : first + P],
-                rhs=h_q[hf][0][:].bitcast(FP8X4),
-                rhs_scale=h_q[hf][1][:],
+                lhsT=w4_codes[:, first : first + P].bitcast(FP4X4),
+                lhsT_scale=w4_plane[g][:, t * P : (t + 1) * P],
+                rhs=codes.bitcast(FP8X4),
+                rhs_scale=plane,
                 start=True,
                 stop=True,
             )
-            if on_vector:
-                nc.vector.tensor_tensor(feat[g, t][:, cols], acc[:], wear_sb[g, t][:, cols], ALU.mult)
-            else:
-                nc.scalar.copy(out=feat[g, t][:, cols], in_=acc[:])
-                nc.gpsimd.tensor_tensor(feat[g, t][:, cols], feat[g, t][:, cols], wear_sb[g, t][:, cols], ALU.mult)
+            nc.vector.tensor_tensor(g2[g, t][:, cols], acc[:], wear_sb[g, t][:, cols], ALU.mult)
 
-        for n, (g, t) in enumerate(rows):
+        for n, (g, t) in enumerate(slices_of_g2):
             features(g, t, 0)
             if n == PACK:
-                h_q.append(quantize(h_rounded[1], "h1"))
+                h_q.append(quantize(h_woven[1], "h1"))
 
-        y_rows = out_0.rearrange("(g p t) m -> g p t m", g=groups, t=PACK)
         steps = [(0, t, 0, M) for t in range(PACK)]
         steps += [(1, t, m0, m0 + M // 2) for m0 in (0, M // 2) for t in range(PACK)]
+        y_rows = out_0.rearrange("(g p t) m -> g p t m", g=groups, t=PACK)
+        y_codes = [keep.tile([P, M], U32, name="y_codes%d" % g, align_bytes=MX_ALIGN) for g in range(groups)]
+        y_plane = [keep.tile([P, M], U8, name="y_plane%d" % g, align_bytes=MX_ALIGN) for g in range(groups)]
 
-        picked = {}
+        def pick_left(g, t, m0, m1):
+            picked = ring.tile([P, m1 - m0], F32, name="picked", tag="picked")
+            nc.vector.tensor_copy(picked[:], g2[g, t][:].indirect(left[:, entries(m0, m1)]))
+            return picked
 
-        def pick_left(g, t):
-            picked[g, t] = wide.tile([P, M], F32, name="picked", tag="picked", bufs=5)
-            nc.vector.tensor_copy(picked[g, t][:], feat[g, t][:].indirect(left[:]))
-
-        features(*rows[0], 1)
-        features(*rows[1], 1)
-        features(*rows[2], 1, on_vector=False)
-        pick_left(*rows[0])
-        y = {}
-        y_codes = [keep.tile([P, M], U32, name="y_codes%d" % g, align_bytes=64) for g in range(groups)]
-        y_plane = [keep.tile([P, M], U8, name="y_plane%d" % g, align_bytes=64) for g in range(groups)]
+        features(*slices_of_g2[0], 1)
+        features(*slices_of_g2[1], 1)
+        next_picked = pick_left(*steps[0])
         for n, (g, t, m0, m1) in enumerate(steps):
-            width = m1 - m0
-            entries = slice(m0 // LIST_ROWS, m1 // LIST_ROWS)
             if t == 0:
-                y[g, m0] = wide.tile([P, PACK, width], F32, name="y", tag="f32x4")
-            if n + 3 < len(rows):
-                features(*rows[n + 3], 1, on_vector=False)
-            if n + 1 < len(rows):
-                pick_left(*rows[n + 1])
-            pair_sum = ring.tile([P, width], F32, name="pair_sum", tag="pair_sum")
-            nc.vector.tensor_tensor(pair_sum[:], feat[g, t][:].indirect(right[:, entries]), picked[g, t][:, m0:m1], ALU.add)
+                y = wide.tile([P, PACK, m1 - m0], F32, name="y", tag="f32x4")
+            picked = next_picked
+            if n + 2 < len(slices_of_g2):
+                features(*slices_of_g2[n + 2], 1)
+            if n + 1 < len(steps):
+                next_picked = pick_left(*steps[n + 1])
+            pair_sum = ring.tile([P, m1 - m0], F32, name="pair_sum", tag="pair_sum")
+            nc.vector.tensor_tensor(pair_sum[:], g2[g, t][:].indirect(right[:, entries(m0, m1)]), picked[:], ALU.add)
             nc.scalar.activation(pair_sum[:], pair_sum[:], ACT.Tanh)
-            nc.scalar.activation(y[g, m0][:, t, :], pair_sum[:], ACT.Copy, scale=gy_sb[:, g, t : t + 1])
+            nc.scalar.activation(y[:, t, :], pair_sum[:], ACT.Copy, scale=gy_sb[:, g, t : t + 1])
             if t % 2:
-                nc.sync.dma_start(out=y_rows[g, :, t - 1 : t + 1, m0:m1], in_=y[g, m0][:, t - 1 : t + 1, :])
+                nc.sync.dma_start(out=y_rows[g, :, t - 1 : t + 1, m0:m1], in_=y[:, t - 1 : t + 1, :])
             if t == PACK - 1:
-                woven = wide.tile([P, PACK * width], BF16, name="woven", tag="bf16x4", align_bytes=64)
-                last = (g, m1) == (groups - 1, M)
-                interleave(nc.vector.tensor_copy if last else nc.scalar.copy, woven[:], y[g, m0][:])
+                last = n == len(steps) - 1
+                woven = weave(nc.vector.tensor_copy if last else nc.scalar.copy, y[:])
                 nc.vector.quantize_mx(
                     out=y_codes[g][:, m0:m1].bitcast(FP8X4), scales=y_plane[g][:, m0:m1], in_=woven[:]
                 )
-                nc.sync.dma_start(
-                    out=out_1[g, :, m0:m1, :].rearrange("p m i -> p (m i)").bitcast(I32),
-                    in_=y_codes[g][:, m0:m1].bitcast(I32),
-                )
+                nc.sync.dma_start(out=words(out_1[g, :, m0:m1, :]), in_=y_codes[g][:, m0:m1].bitcast(I32))
                 if m1 == M:
                     for q in range(QUADS):
                         queue = nc.scalar if last and q % 2 else nc.sync
                         queue.dma_start(
-                            out=out_2[g, 4 * q : 4 * q + 4, :].bitcast(I32),
-                            in_=y_plane[g][32 * q : 32 * q + 4, :].bitcast(I32),
+                            out=out_2[g, scale_rows(q), :].bitcast(I32), in_=quadrant_rows(y_plane[g], q, PLANE_ROWS)
                         )

from contextlib import ExitStack

import concourse.mybir as mybir

K, T, S, H, N, M = 1024, 4096, 1024, 512, 1024, 512
FLOPS = 2 * (3 * K * H * S + H * N * S)

F32 = mybir.dt.float32
BF16 = mybir.dt.bfloat16
I32 = mybir.dt.int32
U32 = mybir.dt.uint32
U16 = mybir.dt.uint16
U8 = mybir.dt.uint8
FP8X4 = mybir.dt.float8_e4m3fn_x4
FP4X4 = mybir.dt.float4_e2m1fn_x4
ALU = mybir.AluOpType
ACT = mybir.ActivationFunctionType

P = 128
PACK = 4
PASS = P * PACK
BANK = 512
LIST_ROWS = 16
QUADS = 4
QUAD = P // QUADS
PLANE_ROWS = 4
LINE = 4
MX_ALIGN = 64


def tile_list_zipper_tooth_features_kernel(
    tc, tab_words, tab_scales, offs, pos1, pos2, w1, w2_words, w2_scales, w3, gh,
    w4_words, w4_scales, wear, gy, out_0, out_1, out_2,
):
    nc = tc.nc
    passes = K // PASS
    halves = S // BANK
    groups = N // PASS

    def words(dram):
        return dram.rearrange("p c i -> p (c i)").bitcast(I32)

    def quadrant_rows(plane, q, count):
        return plane[QUAD * q : QUAD * q + count, :].bitcast(I32)

    def scale_rows(q):
        return slice(PLANE_ROWS * q, PLANE_ROWS * (q + 1))

    def entries(first, last):
        return slice(first // LIST_ROWS, last // LIST_ROWS)

    with ExitStack() as ctx:
        keep = ctx.enter_context(tc.tile_pool(name="keep", bufs=1))
        wide = ctx.enter_context(tc.tile_pool(name="wide", bufs=4))
        ring = ctx.enter_context(tc.tile_pool(name="ring", bufs=3))
        psum = ctx.enter_context(tc.psum_pool(name="psum", bufs=PACK))
        bank_sets = ("low", "high")

        tab_plane = keep.tile([P, T], U8, name="tab_plane", align_bytes=MX_ALIGN)
        w2_plane_raw = keep.tile([P, H], U8, name="w2_plane_raw", align_bytes=MX_ALIGN)
        w4_plane_raw = keep.tile([P, N], U8, name="w4_plane_raw", align_bytes=MX_ALIGN)
        for plane in (tab_plane, w2_plane_raw, w4_plane_raw):
            nc.vector.memset(plane[:].bitcast(I32), 0)

        idx = keep.tile([P, S // LIST_ROWS], U16, name="idx")
        nc.sync.dma_start(idx[:], offs)
        left = keep.tile([P, M // LIST_ROWS], U16, name="left")
        nc.sync.dma_start(left[:], pos1)
        right = keep.tile([P, M // LIST_ROWS], U16, name="right")
        nc.sync.dma_start(right[:], pos2)
        gh_sb = keep.tile([P, PACK], F32, name="gh_sb")
        nc.sync.dma_start(out=gh_sb[:], in_=gh.rearrange("(p t) -> p t", t=PACK))
        gy_sb = keep.tile([P, groups, PACK], F32, name="gy_sb")
        nc.sync.dma_start(out=gy_sb[:], in_=gy.rearrange("(g p t) -> p g t", g=groups, t=PACK))
        w2_raw = [keep.tile([P, H], I32, name="w2_raw%d" % a) for a in range(passes)]
        for a in range(passes):
            nc.sync.dma_start(out=w2_raw[a][:], in_=words(w2_words[a]))

        tab = [keep.tile([P, T], I32, name="tab%d" % a, tag="tab%d" % a, align_bytes=MX_ALIGN) for a in range(passes)]
        nc.sync.dma_start(out=tab[0][:, : T // 2], in_=words(tab_words[0])[:, : T // 2])
        for q in range(QUADS):
            nc.sync.dma_start(
                out=quadrant_rows(tab_plane, q, PLANE_ROWS * passes), in_=tab_scales[:, scale_rows(q), :].bitcast(I32)
            )
        for q in range(QUADS):
            if q == QUADS // 2:
                nc.sync.dma_start(out=tab[0][:, T // 2 :], in_=words(tab_words[0])[:, T // 2 :])
            nc.sync.dma_start(
                out=quadrant_rows(w2_plane_raw, q, PLANE_ROWS * passes), in_=w2_scales[:, scale_rows(q), :].bitcast(I32)
            )
        nc.sync.dma_start(out=tab[1][:], in_=words(tab_words[1]))

        def load_weight(pool, w, a, first, last, tag):
            raw = pool.tile([P, PACK, last - first], F32, name="raw", tag=tag)
            nc.sync.dma_start(
                out=raw[:], in_=w[a * PASS : (a + 1) * PASS, first:last].rearrange("(p i) c -> p i c", i=PACK)
            )
            return raw, first, last

        w1_raw = [
            [load_weight(keep, w1, 0, 0, H, "w1_raw0")],
            [load_weight(keep, w1, 1, c, c + H // 2, "w1_raw1_%d" % c) for c in (0, H // 2)],
        ]
        w3_raw = [[load_weight(wide, w3, a, 0, H, "f32x4")] for a in range(passes)]
        for q in range(QUADS):
            nc.sync.dma_start(
                out=quadrant_rows(w4_plane_raw, q, PLANE_ROWS), in_=w4_scales[0, scale_rows(q), :].bitcast(I32)
            )
        w4_raw = keep.tile([P, N], U16, name="w4_raw")
        nc.sync.dma_start(out=w4_raw[:].bitcast(I32), in_=w4_words[0].bitcast(I32))
        wear_rows = wear.rearrange("(g p t) j -> g p t j", g=groups, t=PACK)
        wear_sb = {}
        for g in range(groups):
            for t in range(0, PACK, 2):
                two_slices = keep.tile([P, 2, S], F32, name="wear%d%d" % (g, t))
                nc.sync.dma_start(out=two_slices[:], in_=wear_rows[g, :, t : t + 2, :])
                wear_sb[g, t] = two_slices[:, 0, :]
                wear_sb[g, t + 1] = two_slices[:, 1, :]

        def deal(out, in_):
            nc.vector.tensor_copy(
                out=out.rearrange("p (g t m) -> p g m t", t=PACK, m=P),
                in_=in_.rearrange("p (g m t) -> p g m t", t=PACK, m=P),
            )

        def round_weight(rounded, pieces, copy):
            dealt = rounded[:].rearrange("p (t m i) -> p m i t", t=PACK, i=PACK)
            for raw, first, last in pieces:
                copy(out=dealt[:, first // PACK : last // PACK], in_=raw[:].rearrange("p i (m t) -> p m i t", t=PACK))
            return rounded

        def weave(copy, slices_in):
            woven = wide.tile([P, PACK * slices_in.shape[2]], BF16, name="woven", tag="bf16x4", align_bytes=MX_ALIGN)
            copy(
                out=woven[:].rearrange("p (c i t) -> p c t i", i=LINE, t=PACK),
                in_=slices_in.rearrange("p t (c i) -> p c t i", i=LINE),
            )
            return woven

        def quantize(rounded, name):
            width = rounded.shape[1] // PACK
            codes = keep.tile([P, width], U32, name=name + "_codes", align_bytes=MX_ALIGN)
            plane = keep.tile([P, width], U8, name=name + "_plane", align_bytes=MX_ALIGN)
            nc.vector.quantize_mx(out=codes[:].bitcast(FP8X4), scales=plane[:], in_=rounded[:])
            return codes[:], plane[:]

        w2_codes = [keep.tile([P, H], I32, name="w2_codes%d" % a, align_bytes=MX_ALIGN) for a in range(passes)]
        for a in range(passes):
            deal(w2_codes[a][:], w2_raw[a][:])

        v_codes = [
            [keep.tile([P, BANK], U32, name="v_codes%d%d" % (a, hf), align_bytes=MX_ALIGN) for hf in range(halves)]
            for a in range(passes)
        ]
        v_plane = [keep.tile([P, BANK], U8, name="v_plane%d" % hf, align_bytes=MX_ALIGN) for hf in range(halves)]
        w2_plane = keep.tile([P, H], U8, name="w2_plane", align_bytes=MX_ALIGN)

        def look_up(out, window, hf):
            nc.vector.tensor_copy(out[hf][:], window.indirect(idx[:, entries(hf * BANK, (hf + 1) * BANK)]))

        for hf in range(halves):
            look_up(v_plane, tab_plane[:], hf)
        look_up(v_codes[0], tab[0][:].bitcast(U32), 0)
        deal(w2_plane[:], w2_plane_raw[:])
        look_up(v_codes[0], tab[0][:].bitcast(U32), 1)
        for hf in range(halves):
            look_up(v_codes[1], tab[1][:].bitcast(U32), hf)

        def response(weight, t, hf, banks):
            acc = psum.tile([P, BANK], F32, name="acc", tag=banks)
            for a, (codes, plane) in enumerate(weight):
                nc.tensor.matmul_mx(
                    out=acc[:],
                    lhsT=codes[:, t * P : (t + 1) * P].bitcast(FP8X4),
                    lhsT_scale=plane[:, t * P : (t + 1) * P],
                    rhs=v_codes[a][hf][:].bitcast(FP8X4),
                    rhs_scale=v_plane[hf][PLANE_ROWS * a : P, :],
                    start=(a == 0),
                    stop=(a == passes - 1),
                )
            return acc

        banks_of_h = [(hf, t) for hf in range(halves) for t in range(PACK)]

        w2_q = [(w2_codes[a][:], w2_plane[PLANE_ROWS * a : P, :]) for a in range(passes)]
        joined = {}
        for hf, t in banks_of_h:
            acc = response(w2_q, t, hf, bank_sets[1])
            joined[hf, t] = keep.tile([P, BANK], F32, name="joined%d%d" % (hf, t))
            nc.scalar.copy(out=joined[hf, t][:], in_=acc[:])

        w1_q = []
        for a in range(passes):
            rounded = keep.tile([P, PACK * H], BF16, name="rounded", tag="tab%d" % (passes - 1 - a), align_bytes=MX_ALIGN)
            w1_q.append(quantize(round_weight(rounded, w1_raw[a], nc.vector.tensor_copy), "w1_%d" % a))
        w3_rounded = []
        for a in range(passes):
            rounded = wide.tile([P, PACK * H], BF16, name="rounded", tag="bf16x4", align_bytes=MX_ALIGN)
            w3_rounded.append(round_weight(rounded, w3_raw[a], nc.scalar.copy))

        w3_q = []
        for n, (hf, t) in enumerate(banks_of_h):
            acc = response(w1_q, t, hf, bank_sets[hf])
            nc.vector.tensor_tensor(joined[hf, t][:], acc[:], joined[hf, t][:], ALU.min)
            if n == len(banks_of_h) - 3:
                w3_q.append(quantize(w3_rounded[0], "w3_0"))
        w3_q.append(quantize(w3_rounded[1], "w3_1"))

        w4_plane = [keep.tile([P, PASS], U8, name="w4_plane%d" % g, align_bytes=MX_ALIGN) for g in range(groups)]
        w4_codes = keep.tile([P, N], U16, name="w4_codes", align_bytes=MX_ALIGN)
        deal(w4_plane[0][:], w4_plane_raw[:, :PASS])
        h_rows = [
            wide.tile([P, PACK, BANK], BF16, name="h_rows", tag="bf16x4", align_bytes=MX_ALIGN) for hf in range(halves)
        ]
        h_woven = []
        h_q = []
        for hf, t in banks_of_h:
            if (hf, t) == banks_of_h[-1]:
                deal(w4_plane[1][:], w4_plane_raw[:, PASS:])
                deal(w4_codes[:], w4_raw[:])
                h_q.append(quantize(h_woven[0], "h0"))
            acc = response(w3_q, t, hf, bank_sets[hf])
            nc.vector.tensor_tensor(joined[hf, t][:], acc[:], joined[hf, t][:], ALU.max)
            nc.scalar.activation(h_rows[hf][:, t, :], joined[hf, t][:], ACT.Copy, scale=gh_sb[:, t : t + 1])
            if t == PACK - 1:
                h_woven.append(weave(nc.scalar.copy, h_rows[hf][:]))

        slices_of_g2 = [(g, t) for g in range(groups) for t in range(PACK)]
        g2 = {gt: keep.tile([P, S], F32, name="g2_%d%d" % gt) for gt in slices_of_g2}

        def features(g, t, hf):
            acc = psum.tile([P, BANK], F32, name="acc", tag=bank_sets[0])
            first = (g * PACK + t) * P
            cols = slice(hf * BANK, (hf + 1) * BANK)
            codes, plane = h_q[hf]
            nc.tensor.matmul_mx(
                out=acc[:],
                lhsT=w4_codes[:, first : first + P].bitcast(FP4X4),
                lhsT_scale=w4_plane[g][:, t * P : (t + 1) * P],
                rhs=codes.bitcast(FP8X4),
                rhs_scale=plane,
                start=True,
                stop=True,
            )
            nc.vector.tensor_tensor(g2[g, t][:, cols], acc[:], wear_sb[g, t][:, cols], ALU.mult)

        for n, (g, t) in enumerate(slices_of_g2):
            features(g, t, 0)
            if n == PACK:
                h_q.append(quantize(h_woven[1], "h1"))

        steps = [(0, t, 0, M) for t in range(PACK)]
        steps += [(1, t, m0, m0 + M // 2) for m0 in (0, M // 2) for t in range(PACK)]
        y_rows = out_0.rearrange("(g p t) m -> g p t m", g=groups, t=PACK)
        y_codes = [keep.tile([P, M], U32, name="y_codes%d" % g, align_bytes=MX_ALIGN) for g in range(groups)]
        y_plane = [keep.tile([P, M], U8, name="y_plane%d" % g, align_bytes=MX_ALIGN) for g in range(groups)]

        def pick_left(g, t, m0, m1):
            picked = ring.tile([P, m1 - m0], F32, name="picked", tag="picked")
            nc.vector.tensor_copy(picked[:], g2[g, t][:].indirect(left[:, entries(m0, m1)]))
            return picked

        features(*slices_of_g2[0], 1)
        features(*slices_of_g2[1], 1)
        next_picked = pick_left(*steps[0])
        for n, (g, t, m0, m1) in enumerate(steps):
            if t == 0:
                y = wide.tile([P, PACK, m1 - m0], F32, name="y", tag="f32x4")
            picked = next_picked
            if n + 2 < len(slices_of_g2):
                features(*slices_of_g2[n + 2], 1)
            if n + 1 < len(steps):
                next_picked = pick_left(*steps[n + 1])
            pair_sum = ring.tile([P, m1 - m0], F32, name="pair_sum", tag="pair_sum")
            nc.vector.tensor_tensor(pair_sum[:], g2[g, t][:].indirect(right[:, entries(m0, m1)]), picked[:], ALU.add)
            nc.scalar.activation(pair_sum[:], pair_sum[:], ACT.Tanh)
            nc.scalar.activation(y[:, t, :], pair_sum[:], ACT.Copy, scale=gy_sb[:, g, t : t + 1])
            if t % 2:
                nc.sync.dma_start(out=y_rows[g, :, t - 1 : t + 1, m0:m1], in_=y[:, t - 1 : t + 1, :])
            if t == PACK - 1:
                last = n == len(steps) - 1
                woven = weave(nc.vector.tensor_copy if last else nc.scalar.copy, y[:])
                nc.vector.quantize_mx(
                    out=y_codes[g][:, m0:m1].bitcast(FP8X4), scales=y_plane[g][:, m0:m1], in_=woven[:]
                )
                nc.sync.dma_start(out=words(out_1[g, :, m0:m1, :]), in_=y_codes[g][:, m0:m1].bitcast(I32))
                if m1 == M:
                    for q in range(QUADS):
                        queue = nc.scalar if last and q % 2 else nc.sync
                        queue.dma_start(
                            out=out_2[g, scale_rows(q), :].bitcast(I32), in_=quadrant_rows(y_plane[g], q, PLANE_ROWS)
                        )
